import numpy as np, ml_dtypes
CORES = [33,38,57,62,81,86,161,166,185,190,209,214]
N = 12
import mx_ref
NC, G = 128, 4
C = np.float32(0.023)
BF = ml_dtypes.bfloat16
def cut(t, i, w=512):
    return t[:, w * i:w * i + w]
def tile(rs):
    return np.stack(rs, axis=2).reshape(128, -1).astype(BF)
def layer(w, X):
    out = []
    for i in range(G):
        for t in range(len(X)):
            p = mx_ref.matmul(mx_ref.quantize(cut(w, len(X) * i + t)), X[t])
            z = p if t == 0 else z + p
        out.append(z)
    return out
def masked(A, E):
    return [(e * (a > 0)) * C for a, e in zip(A, E)]
def setup_inputs(rng):
    def f(*shape):
        return mx_ref.flush((rng.standard_normal(shape, dtype=np.float32) * np.exp2(rng.integers(-2, 3, shape[:-1] + (1,)))).astype(BF))
    return {"x": f(N, 128, 512), "e": f(N, 128, 512), "a": f(N, 128, G * 512), "v": f(N, 128, 4 * NC)}
def setup_inputs_blocks(rng):
    d = setup_inputs(rng)
    for k in ("x", "e", "a", "v"): d[k] = mx_ref.spread(d[k], rng, 4)
    return d
def setup_inputs_wide(rng):
    d = setup_inputs(rng)
    for k in ("x", "e", "a", "v"): d[k] = mx_ref.flush((d[k].astype(np.float32) * np.exp2(rng.integers(-6, 7, (N, 1, 1))).astype(np.float32)).astype(BF))
    return d
def setup_inputs_zeros(rng):
    d = setup_inputs(rng); v = d["x"].reshape(N, 128, -1, 4).copy()
    v[np.broadcast_to((rng.random((N, 1, v.shape[2], 1)) < 0.33), v.shape)] = 0
    d["x"] = v.reshape(d["x"].shape)
    return d
def reference(x, e, a, v):
    T = [mx_ref.quantize(tile(masked(layer(a[j], [mx_ref.quantize(x[j])]), layer(a[j], [mx_ref.quantize(e[j])])))) for j in range(N)]
    y = np.zeros((N, 128, N * NC), np.float32)
    for r in range(N):
        qv = mx_ref.quantize(v[r])
        for j in range(N):
            y[r][:, NC * j:NC * j + NC] = mx_ref.matmul(T[j], qv)
    return {"y": y}

import numpy as np
from concourse.bass import DstId, RemoteDMATransfer
from concourse.mybir import dt, AluOpType, ActivationFunctionType

WORLD = 256
N = 12
G = 4
W = 128
E = 4 * W
BANK = 512
NBANK = 8
C = float(np.float32(0.023))

PER_RELAY = 2
FIRST_BATCH = 3
HOP = 2.5

SCRATCH = {
    "xe": ("sbuf", [128, 2 * E], "bfloat16"),
    "ab": ("sbuf", [128, G * E], "bfloat16"),
    "vb": ("sbuf", [128, E], "bfloat16"),
    "tb": ("sbuf", [128, E], "bfloat16"),
    "mc": ("sbuf", [128, G * W], "float32"),
    "xq": ("sbuf", [128, 2 * W], "float8_e4m3fn_x4"), "xpl": ("sbuf", [128, 2 * W], "uint8"),
    "aq": ("sbuf", [128, G * W], "float8_e4m3fn_x4"), "apl": ("sbuf", [128, G * W], "uint8"),
    "vq": ("sbuf", [128, W], "float8_e4m3fn_x4"), "vpl": ("sbuf", [128, W], "uint8"),
    "tq": ("sbuf", [128, N * W], "float8_e4m3fn_x4"), "tpl": ("sbuf", [128, N * W], "uint8"),
    "ysb": ("sbuf", [128, N * W], "float32"),
    "ps": ("psum", [128, NBANK * BANK], "float32"),
}
SEMAPHORES = (["lxe", "lv", "qx", "qt", "qv", "tt", "fs", "fc0", "fc1", "sta", "stb", "sent"]
              + ["%s%d" % (n, i) for n in ("la", "qa", "mu", "md", "mk") for i in range(G)]
              + ["sg%d" % i for i in range(G - 1)]
              + ["%s%d" % (n, j) for n in ("sc", "cd", "mm", "cp") for j in range(N)])

_CACHE = {}


def _bits(m):
    return bin(m).count("1")


def _plan(cores, topo):
    if "p" in _CACHE:
        return _CACHE["p"]

    def place(c):
        return (topo.host(c), topo.chip(c))
    chips = sorted(set(place(c) for c in cores))
    K = len(chips)
    kof = dict((c, chips.index(place(c))) for c in cores)
    dies = sorted(set(topo.die(c) for c in cores))
    at = dict(((kof[c], topo.die(c)), c) for c in cores)
    first = {}
    relay = {}
    eta = {}
    for j, c in enumerate(cores):
        k, d = kof[c], topo.die(c)
        others = sorted((q for q in range(K) if q != k), key=lambda q: (q - k) % K)
        near = [at[(q, d)] for q in others if topo.may_write(c, at[(q, d)])]
        far = [at[(q, d)] for q in others if not topo.may_write(c, at[(q, d)])]
        mine = [w for w in range(WORLD) if place(w) == place(c) and topo.die(w) == d and w not in cores
                and all(topo.may_write(w, f) for f in far)]
        nh = min(len(mine), -(-len(far) // PER_RELAY))
        for i in range(nh):
            relay[mine[i]] = (j, far[i::nh])
            for p, f in enumerate(far[i::nh]):
                eta[(f, j)] = HOP + p + 1 + 0.1 * i
        for p, f in enumerate(near):
            eta[(f, j)] = p + 1
        first[c] = (near, mine[:nh] + [p for p in cores if place(p) == place(c) and p != c])
    slot, passes = {}, {}
    for c in cores:
        k, base = kof[c], K * dies.index(topo.die(c))
        got = sorted((j for j in range(len(cores)) if (c, j) in eta), key=lambda j: (eta[(c, j)], j))
        slot[(k, cores.index(c))] = base
        for i, j in enumerate(got):
            slot[(k, j)] = base + 1 + i
        passes[c] = got
    _CACHE["p"] = dict(place=place, chips=chips, kof=kof, first=first, relay=relay, eta=eta, slot=slot, passes=passes)
    return _CACHE["p"]


def _codes(T, s, n=1):
    return T.tq[:, W * s:W * (s + n)].bitcast(dt.uint8)


def _plane(T, s, n=1):
    return T.tpl[:, W * s:W * (s + n)]


def _push(g, T, topo, core, view, groups):
    tr, n_local = [], 0
    for mask, sem, s, n, dsts in groups:
        ids = []
        for d, _ in dsts:
            rid, pid = topo.addr(d, core)
            ids.append(DstId(rid=rid, pnc=pid))
        tr.append(RemoteDMATransfer(dst_ids=ids, dma_engine_mask=mask, remote_sem=sem, srcs=[view(T, s, n)],
                                    dsts=[view(T, ds, n) for _, ds in dsts]))
        n_local += _bits(mask)
    g.remote_dma_fused(tr, local_sem=T.sem.sent)
    return n_local


def _common_mask(topo, core, dsts):
    m = topo.mask(core, dsts[0])
    for d in dsts[1:]:
        m &= topo.mask(core, d)
    return m


def _relay_program(g, core, T, topo, P, cores):
    j, dsts = P["relay"][core]
    src = cores[j]
    here = P["slot"][(P["kof"][src], j)]
    n_in = _bits(_common_mask(topo, src, P["first"][src][1]) & ~_common_mask(topo, src, P["first"][src][0]))
    mask = _common_mask(topo, core, dsts)
    to = [(d, P["slot"][(P["kof"][d], j)]) for d in dsts]
    sent = 0
    for name, view in (("sc", _plane), ("cd", _codes)):
        sem = T.sem["%s%d" % (name, j)]
        g.wait_ge(sem, n_in)
        sent += _push(g, T, topo, core, view, [(mask, sem, here, 1, to)])
    g.wait_ge(T.sem.sent, sent)


def rank_program(g, core, T, topo):
    cores = [int(c) for c in T.cores]
    P = _plan(cores, topo)
    if core in P["relay"]:
        _relay_program(g, core, T, topo, P, cores)
        return
    me = T.rank_of(core)
    if me is None:
        return
    S, v, s, t, sy = T.sem, g.vector, g.scalar, g.tensor, g.sync
    k, slot = P["kof"][core], P["slot"]
    near, local = P["first"][core]
    mate_rank = local[-1]
    off_mask = _common_mask(topo, core, near)
    on_mask = _common_mask(topo, core, local) & ~off_mask
    all_mask = topo.mask(core, mate_rank)
    own = slot[(k, me)]

    sy.dma_start(T.xe[:, 0:E], T.x[:, :]).then_inc(S.lxe, 16)
    s.dma_start(T.xe[:, E:2 * E], T.e[:, :]).then_inc(S.lxe, 16)
    for i in range(G):
        (sy if i % 2 == 0 else s).dma_start(T.ab[:, E * i:E * (i + 1)], T.a[:, E * i:E * (i + 1)]).then_inc(S["la%d" % i], 16)
    sy.dma_start(T.vb[:, :], T.v[:, :]).then_inc(S.lv, 16)

    def bank(b):
        return T.ps[:, BANK * b:BANK * b + W]
    t.wait_ge(S.qx, 1)
    for i in range(G):
        t.wait_ge(S["qa%d" % i], 1)
        for h, name in enumerate(("mu", "md")):
            t.matmul_mx(bank(2 * i + h), T.aq[:, W * i:W * (i + 1)], T.apl[:, W * i:W * (i + 1)],
                        T.xq[:, W * h:W * (h + 1)], T.xpl[:, W * h:W * (h + 1)], True, True).then_inc(S["%s%d" % (name, i)], 1)

    def mc(b):
        return T.mc[:, W * b:W * (b + 1)]
    for b in range(G - 1):
        s.wait_ge(S["mu%d" % b], 1)
        s.activation(mc(b), bank(2 * b), ActivationFunctionType.Sign).then_inc(S["sg%d" % b], 1)
        s.wait_ge(S["sg%d" % b], 1)
        s.activation(mc(b), mc(b), ActivationFunctionType.Relu, scale=C).then_inc(S["mk%d" % b], 1)

    def quant_a(i):
        v.wait_ge(S["la%d" % i], 16)
        v.quantize_mx(T.aq[:, W * i:W * (i + 1)], T.apl[:, W * i:W * (i + 1)], T.ab[:, E * i:E * (i + 1)]).then_inc(S["qa%d" % i], 1)

    def masked(b):
        v.wait_ge(S["md%d" % b], 1)
        v.wait_ge(S["mk%d" % b], 1)
        v.tensor_tensor(T.tb[:, b:E:G], bank(2 * b + 1), mc(b), AluOpType.mult).then_inc(S.tt, 1)
    v.wait_ge(S.lxe, 32)
    v.quantize_mx(T.xq[:, :], T.xpl[:, :], T.xe[:, :]).then_inc(S.qx, 1)
    quant_a(0)
    for i in range(1, G):
        quant_a(i)
        masked(i - 1)
    v.wait_ge(S["mu%d" % (G - 1)], 1)
    v.tensor_scalar(mc(G - 1), bank(2 * (G - 1)), 0.0, C, AluOpType.is_gt, AluOpType.mult).then_inc(S["mk%d" % (G - 1)], 1)
    masked(G - 1)
    v.wait_ge(S.tt, G)
    v.quantize_mx(T.tq[:, W * own:W * (own + 1)], T.tpl[:, W * own:W * (own + 1)], T.tb[:, :]).then_inc(S.qt, 1)
    v.wait_ge(S.lv, 16)
    v.quantize_mx(T.vq[:, :], T.vpl[:, :], T.vb[:, :]).then_inc(S.qv, 1)

    sent = 0
    g.wait_ge(S.qt, 1)
    for name, view in (("sc", _plane), ("cd", _codes)):
        sem = S["%s%d" % (name, me)]
        sent += _push(g, T, topo, core, view, [
            (off_mask, sem, own, 1, [(d, slot[(P["kof"][d], me)]) for d in near]),
            (on_mask, sem, own, 1, [(d, own) for d in local])])
    n_off, n_on, n_all = _bits(off_mask), _bits(on_mask), _bits(all_mask)
    got = P["passes"][core]
    batches = [got[:FIRST_BATCH], got[FIRST_BATCH:]]
    for j in got:
        g.wait_ge(S["sc%d" % j], n_off)
    sent += _push(g, T, topo, core, _plane, [(all_mask, S.fs, slot[(k, got[0])], len(got), [(mate_rank, slot[(k, got[0])])])])
    for b, batch in enumerate(batches):
        for j in batch:
            g.wait_ge(S["cd%d" % j], n_off)
        sent += _push(g, T, topo, core, _codes,
                      [(all_mask, S["fc%d" % b], slot[(k, batch[0])], len(batch), [(mate_rank, slot[(k, batch[0])])])])
    g.wait_ge(S.sent, sent)

    theirs = P["passes"][mate_rank]
    work = [(me, [(S.qt, 1), (S.qv, 1)])]
    jm = cores.index(mate_rank)
    work.append((jm, [(S["sc%d" % jm], n_on), (S["cd%d" % jm], n_on)]))
    for j in got:
        work.append((j, [(S["sc%d" % j], n_off), (S["cd%d" % j], n_off)]))
    for b, batch in enumerate([theirs[:FIRST_BATCH], theirs[FIRST_BATCH:]]):
        for i, j in enumerate(batch):
            work.append((j, ([(S.fs, n_all)] if b == 0 and i == 0 else []) + ([(S["fc%d" % b], n_all)] if i == 0 else [])))
    stores = [0, 0]
    for m, (j, waits) in enumerate(work):
        for sem, n in waits:
            t.wait_ge(sem, n)
        if m >= NBANK:
            t.wait_ge(S["cp%d" % (m - NBANK)], 1)
        q = slot[(k, j)]
        t.matmul_mx(bank(m % NBANK), T.tq[:, W * q:W * (q + 1)], T.tpl[:, W * q:W * (q + 1)], T.vq[:, :], T.vpl[:, :],
                    True, True).then_inc(S["mm%d" % m], 1)
        out = T.ysb[:, W * j:W * (j + 1)]
        if m % 2 == 0:
            v.wait_ge(S["mm%d" % m], 1)
            v.tensor_copy(out, bank(m % NBANK)).then_inc(S["cp%d" % m], 1)
        else:
            s.wait_ge(S["mm%d" % m], 1)
            s.activation(out, bank(m % NBANK), ActivationFunctionType.Copy).then_inc(S["cp%d" % m], 1)
        dq = sy if m % 2 == 0 else s
        dq.wait_ge(S["cp%d" % m], 1)
        dq.dma_start(T.y[:, W * j:W * (j + 1)], out).then_inc(S.sta if m % 2 == 0 else S.stb, 16)
        stores[m % 2] += 16
    sy.wait_ge(S.sta, stores[0])
    s.wait_ge(S.stb, stores[1])
